import numpy as np
CORES = [0,1,2,3,4,5,6,7,8,9,10,11,12,13,14,15,16,17,18,19,20,21,22,23,24,25,26,27,28,29,30,31,32,33,34,35,36,37,38,39,40,41,42,43,44,45,46,47,48,49,50,51,52,53,54,55,56,57,58,59,60,61,62,63,64,65,66,67,68,69,70,71,72,73,74,75,76,77,78,79,80,81,82,83,84,85,86,87,88,89,90,91,92,93,94,95,96,97,98,99,100,101,102,103,104,105,106,107,108,109,110,111,112,113,114,115,116,117,118,119,120,121,122,123,124,125,126,127,128,129,130,131,132,133,134,135,136,137,138,139,140,141,142,143,144,145,146,147,148,149,150,151,152,153,154,155,156,157,158,159,160,161,162,163,164,165,166,167,168,169,170,171,172,173,174,175,176,177,178,179,180,181,182,183,184,185,186,187,188,189,190,191,192,193,194,195,196,197,198,199,200,201,202,203,204,205,206,207,208,209,210,211,212,213,214,215,216,217,218,219,220,221,222,223,224,225,226,227,228,229,230,231,232,233,234,235,236,237,238,239,240,241,242,243,244,245,246,247,248,249,250,251,252,253,254,255]
N = 256
PERM = [[j, 128 + (5 * j + 3) % 128] for j in range(128)] + [[128 + (5 * j + 3) % 128, j] for j in range(128)]
def setup_inputs(rng):
    return {"x": rng.standard_normal((N, 128, 512), dtype=np.float32)}
def reference(x):
    y = np.empty_like(x)
    for s, d in PERM:
        y[d] = x[s]
    return {"y": y}

@@ -1,0 +1,89 @@
+from concourse.bass import DstId, RemoteDMATransfer
+
+WIDTH = 512
+HALF = WIDTH // 2
+
+SCRATCH = {
+    "send": ("sbuf", [128, WIDTH], "float32"),
+    "pass_on": ("sbuf", [128, WIDTH], "float32"),
+    "land": ("sbuf", [128, WIDTH], "float32"),
+}
+SEMAPHORES = ["loaded", "passed", "arrived", "sent", "stored"]
+
+WHOLE_DIRECT = [(0, WIDTH, None)]
+ROUTE = {
+    0: {1: [(0, HALF, 3), (HALF, WIDTH, 6)],
+        4: [(0, HALF, None), (HALF, WIDTH, 0)],
+        5: [(0, WIDTH, 7)]},
+    1: {0: [(0, WIDTH, 2)],
+        1: [(0, HALF, None), (HALF, WIDTH, 5)],
+        4: [(0, HALF, 3), (HALF, WIDTH, 6)],
+        5: [(0, WIDTH, 7)]},
+}
+
+LOW8, HIGH8, ALL16 = 0x00FF, 0xFF00, 0xFFFF
+
+
+def engines(mask):
+    return bin(mask).count("1")
+
+
+def pieces_of(core, topo):
+    table = ROUTE[topo.host(core)].get(core % 8, WHOLE_DIRECT)
+    out = []
+    for i, (lo, hi, via) in enumerate(table):
+        carrier = None if via is None else core - core % 8 + via
+        if len(table) == 1:
+            mask = LOW8 if carrier is None else ALL16
+        else:
+            mask = LOW8 if i == 0 else HIGH8
+        out.append((lo, hi, carrier, mask))
+    return out
+
+
+def rank_program(g, core, T, topo):
+    rank = T.rank_of(core)
+    if rank is None:
+        return
+    to = {T.cores[s]: T.cores[d] for s, d in T.perm}
+    frm = {d: s for s, d in to.items()}
+    sem = T.sem
+    sent = 0
+
+    g.dma_start(T.send[:], T.x[:]).then_inc(sem.loaded, 16)
+    g.wait_ge(sem.loaded, 16)
+
+    transfers = []
+    for lo, hi, carrier, mask in pieces_of(core, topo):
+        if carrier is None:
+            dst, buf, rsem = to[core], T.land, sem.arrived
+        else:
+            dst, buf, rsem = carrier, T.pass_on, sem.passed
+        rid, pid = topo.addr(dst, core)
+        transfers.append((buf[:, lo:hi], T.send[:, lo:hi], rsem, pid, rid, mask))
+        sent += engines(mask)
+    if len(transfers) == 1:
+        out_ap, in_ap, rsem, pid, rid, mask = transfers[0]
+        g.remote_dma(out_ap, in_ap, rsem, sem.sent, pid, rid, mask)
+    else:
+        g.remote_dma_fused(
+            [RemoteDMATransfer(dst_ids=[DstId(rid=rid, pnc=pid)], dma_engine_mask=mask, remote_sem=rsem,
+                               src=in_ap, dst=out_ap)
+             for out_ap, in_ap, rsem, pid, rid, mask in transfers],
+            local_sem=sem.sent)
+
+    chip0 = core - core % 8
+    for owner in range(chip0, chip0 + 8):
+        for lo, hi, carrier, mask in pieces_of(owner, topo):
+            if carrier != core:
+                continue
+            g.wait_ge(sem.passed, engines(mask))
+            rid, pid = topo.addr(to[owner], core)
+            g.remote_dma(T.land[:, lo:hi], T.pass_on[:, lo:hi], sem.arrived, sem.sent, pid, rid, LOW8)
+            sent += engines(LOW8)
+
+    g.wait_ge(sem.arrived, engines(LOW8) * len(pieces_of(frm[core], topo)))
+    g.dma_start(T.y[:], T.land[:]).then_inc(sem.stored, 16)
+
+    g.wait_ge(sem.sent, sent)
+    g.wait_ge(sem.stored, 16)

@@ -4,21 +4,24 @@ WIDTH = 512
 HALF = WIDTH // 2
 
 SCRATCH = {
-    "send": ("sbuf", [128, WIDTH], "float32"),
-    "pass_on": ("sbuf", [128, WIDTH], "float32"),
-    "land": ("sbuf", [128, WIDTH], "float32"),
+    "send_w": ("dram", [128, WIDTH], "float32"),
+    "send_h": ("dram", [2, 128, HALF], "float32"),
+    "pass_w": ("dram", [128, WIDTH], "float32"),
+    "pass_h": ("dram", [128, HALF], "float32"),
+    "land_w": ("dram", [128, WIDTH], "float32"),
+    "land_h": ("dram", [2, 128, HALF], "float32"),
 }
 SEMAPHORES = ["loaded", "passed", "arrived", "sent", "stored"]
 
-WHOLE_DIRECT = [(0, WIDTH, None)]
+WHOLE_DIRECT = [None]
 ROUTE = {
-    0: {1: [(0, HALF, 3), (HALF, WIDTH, 6)],
-        4: [(0, HALF, None), (HALF, WIDTH, 0)],
-        5: [(0, WIDTH, 7)]},
-    1: {0: [(0, WIDTH, 2)],
-        1: [(0, HALF, None), (HALF, WIDTH, 5)],
-        4: [(0, HALF, 3), (HALF, WIDTH, 6)],
-        5: [(0, WIDTH, 7)]},
+    0: {1: [3, 6],
+        4: [None, 0],
+        5: [7]},
+    1: {0: [2],
+        1: [None, 5],
+        4: [3, 7],
+        5: [6]},
 }
 
 LOW8, HIGH8, ALL16 = 0x00FF, 0xFF00, 0xFFFF
@@ -31,13 +34,13 @@ def engines(mask):
 def pieces_of(core, topo):
     table = ROUTE[topo.host(core)].get(core % 8, WHOLE_DIRECT)
     out = []
-    for i, (lo, hi, via) in enumerate(table):
+    for i, via in enumerate(table):
         carrier = None if via is None else core - core % 8 + via
         if len(table) == 1:
             mask = LOW8 if carrier is None else ALL16
         else:
             mask = LOW8 if i == 0 else HIGH8
-        out.append((lo, hi, carrier, mask))
+        out.append((carrier, mask))
     return out
 
 
@@ -50,19 +53,24 @@ def rank_program(g, core, T, topo):
     sem = T.sem
     sent = 0
 
-    g.dma_start(T.send[:], T.x[:]).then_inc(sem.loaded, 16)
+    def part(whole, halves, n, i):
+        return whole[:] if n == 1 else halves[i]
+
+    mine = pieces_of(core, topo)
+    n = len(mine)
+    g.dma_start(T.send_w[:] if n == 1 else T.send_h[:], T.x[:]).then_inc(sem.loaded, 16)
     g.wait_ge(sem.loaded, 16)
 
     transfers = []
-    for lo, hi, carrier, mask in pieces_of(core, topo):
+    for i, (carrier, mask) in enumerate(mine):
         if carrier is None:
-            dst, buf, rsem = to[core], T.land, sem.arrived
+            dst, out_ap, rsem = to[core], part(T.land_w, T.land_h, n, i), sem.arrived
         else:
-            dst, buf, rsem = carrier, T.pass_on, sem.passed
+            dst, out_ap, rsem = carrier, (T.pass_w[:] if n == 1 else T.pass_h[:]), sem.passed
         rid, pid = topo.addr(dst, core)
-        transfers.append((buf[:, lo:hi], T.send[:, lo:hi], rsem, pid, rid, mask))
+        transfers.append((out_ap, part(T.send_w, T.send_h, n, i), rsem, pid, rid, mask))
         sent += engines(mask)
-    if len(transfers) == 1:
+    if n == 1:
         out_ap, in_ap, rsem, pid, rid, mask = transfers[0]
         g.remote_dma(out_ap, in_ap, rsem, sem.sent, pid, rid, mask)
     else:
@@ -74,16 +82,20 @@ def rank_program(g, core, T, topo):
 
     chip0 = core - core % 8
     for owner in range(chip0, chip0 + 8):
-        for lo, hi, carrier, mask in pieces_of(owner, topo):
+        theirs = pieces_of(owner, topo)
+        for i, (carrier, mask) in enumerate(theirs):
             if carrier != core:
                 continue
             g.wait_ge(sem.passed, engines(mask))
             rid, pid = topo.addr(to[owner], core)
-            g.remote_dma(T.land[:, lo:hi], T.pass_on[:, lo:hi], sem.arrived, sem.sent, pid, rid, LOW8)
+            g.remote_dma(part(T.land_w, T.land_h, len(theirs), i),
+                         T.pass_w[:] if len(theirs) == 1 else T.pass_h[:],
+                         sem.arrived, sem.sent, pid, rid, LOW8)
             sent += engines(LOW8)
 
-    g.wait_ge(sem.arrived, engines(LOW8) * len(pieces_of(frm[core], topo)))
-    g.dma_start(T.y[:], T.land[:]).then_inc(sem.stored, 16)
+    m = len(pieces_of(frm[core], topo))
+    g.wait_ge(sem.arrived, engines(LOW8) * m)
+    g.dma_start(T.y[:], T.land_w[:] if m == 1 else T.land_h[:]).then_inc(sem.stored, 16)
 
     g.wait_ge(sem.sent, sent)
     g.wait_ge(sem.stored, 16)

from concourse.bass import DstId, RemoteDMATransfer

WIDTH = 512
HALF = WIDTH // 2

SCRATCH = {
    "send_w": ("dram", [128, WIDTH], "float32"),
    "send_h": ("dram", [2, 128, HALF], "float32"),
    "pass_w": ("dram", [128, WIDTH], "float32"),
    "pass_h": ("dram", [128, HALF], "float32"),
    "land_w": ("dram", [128, WIDTH], "float32"),
    "land_h": ("dram", [2, 128, HALF], "float32"),
}
SEMAPHORES = ["loaded", "passed", "arrived", "sent", "stored"]

WHOLE_DIRECT = [None]
ROUTE = {
    0: {1: [3, 6],
        4: [None, 0],
        5: [7]},
    1: {0: [2],
        1: [None, 5],
        4: [3, 7],
        5: [6]},
}

LOW8, HIGH8, ALL16 = 0x00FF, 0xFF00, 0xFFFF


def engines(mask):
    return bin(mask).count("1")


def pieces_of(core, topo):
    table = ROUTE[topo.host(core)].get(core % 8, WHOLE_DIRECT)
    out = []
    for i, via in enumerate(table):
        carrier = None if via is None else core - core % 8 + via
        if len(table) == 1:
            mask = LOW8 if carrier is None else ALL16
        else:
            mask = LOW8 if i == 0 else HIGH8
        out.append((carrier, mask))
    return out


def rank_program(g, core, T, topo):
    rank = T.rank_of(core)
    if rank is None:
        return
    to = {T.cores[s]: T.cores[d] for s, d in T.perm}
    frm = {d: s for s, d in to.items()}
    sem = T.sem
    sent = 0

    def part(whole, halves, n, i):
        return whole[:] if n == 1 else halves[i]

    mine = pieces_of(core, topo)
    n = len(mine)
    g.dma_start(T.send_w[:] if n == 1 else T.send_h[:], T.x[:]).then_inc(sem.loaded, 16)
    g.wait_ge(sem.loaded, 16)

    transfers = []
    for i, (carrier, mask) in enumerate(mine):
        if carrier is None:
            dst, out_ap, rsem = to[core], part(T.land_w, T.land_h, n, i), sem.arrived
        else:
            dst, out_ap, rsem = carrier, (T.pass_w[:] if n == 1 else T.pass_h[:]), sem.passed
        rid, pid = topo.addr(dst, core)
        transfers.append((out_ap, part(T.send_w, T.send_h, n, i), rsem, pid, rid, mask))
        sent += engines(mask)
    if n == 1:
        out_ap, in_ap, rsem, pid, rid, mask = transfers[0]
        g.remote_dma(out_ap, in_ap, rsem, sem.sent, pid, rid, mask)
    else:
        g.remote_dma_fused(
            [RemoteDMATransfer(dst_ids=[DstId(rid=rid, pnc=pid)], dma_engine_mask=mask, remote_sem=rsem,
                               src=in_ap, dst=out_ap)
             for out_ap, in_ap, rsem, pid, rid, mask in transfers],
            local_sem=sem.sent)

    chip0 = core - core % 8
    for owner in range(chip0, chip0 + 8):
        theirs = pieces_of(owner, topo)
        for i, (carrier, mask) in enumerate(theirs):
            if carrier != core:
                continue
            g.wait_ge(sem.passed, engines(mask))
            rid, pid = topo.addr(to[owner], core)
            g.remote_dma(part(T.land_w, T.land_h, len(theirs), i),
                         T.pass_w[:] if len(theirs) == 1 else T.pass_h[:],
                         sem.arrived, sem.sent, pid, rid, LOW8)
            sent += engines(LOW8)

    m = len(pieces_of(frm[core], topo))
    g.wait_ge(sem.arrived, engines(LOW8) * m)
    g.dma_start(T.y[:], T.land_w[:] if m == 1 else T.land_h[:]).then_inc(sem.stored, 16)

    g.wait_ge(sem.sent, sent)
    g.wait_ge(sem.stored, 16)
